import numpy as np
import ml_dtypes


def mxq(x, axis, fmt="e4m3"):
    dtype, down = {"e4m3": (ml_dtypes.float8_e4m3fn, 7), "e5m2": (ml_dtypes.float8_e5m2, 14)}[fmt]
    v = np.moveaxis(np.asarray(x, np.float32).astype(ml_dtypes.bfloat16).astype(np.float64), axis, -1)
    blocks = v.reshape(v.shape[:-1] + (-1, 32))
    amax = np.abs(blocks).max(-1, keepdims=True)
    byte = np.maximum(np.where(amax > 0, np.frexp(amax)[1] - 1 + 127, 0) - down, 1)
    scale = np.exp2(byte - 127.0)
    codes = (blocks / scale).astype(np.float32).astype(dtype).astype(np.float64)
    return np.moveaxis((codes * scale).reshape(v.shape), -1, axis)


WIDE = False


def mx_kscale(k):
    if not WIDE:
        return np.ones(k)
    levels = np.array([10, -10, 5, -5, 0])
    if k % 512:
        return np.exp2(np.random.permutation(np.resize(levels, k // 32))).repeat(32)
    a = np.empty((k // 512, 16))
    for p in range(k // 512):
        a[p, :8] = np.random.permutation(np.resize(levels, 8))
        for g in range(8):
            far = levels[np.abs(levels - a[p, g]) >= 10]
            a[p, g + 8] = far[np.random.randint(len(far))]
    return np.exp2(a.ravel()).repeat(32)


def f64(x):
    return np.asarray(x).astype(np.float64)


def striped(idx):
    return np.tile(idx.reshape(-1, 16).T, (8, 1)).astype(np.uint16)


def unstriped(offs):
    return offs[:16].T.reshape(-1).astype(np.int64)


def striped8(idx):
    return np.concatenate([x.reshape(-1, 16).T for x in idx]).astype(np.uint16)


def runs(offs, k):
    lists = np.stack([offs[16 * r : 16 * r + 16].T.reshape(-1) for r in range(8)]).astype(np.int64)
    return lists[np.arange(k) % 512 // 64]


def pack_weight(w):
    k, n = w.shape
    w = f64(np.asarray(w, np.float32).astype(ml_dtypes.bfloat16)).reshape(k // 32, 32, n)
    amax = np.abs(w).max(1)
    byte = np.clip(np.where(amax > 0, np.frexp(amax)[1] - 1 + 127 - 7, 1), 1, 254)
    scaled = (w * np.exp2(127.0 - byte)[:, None, :]).reshape(k, n).astype(np.float32)
    words = np.ascontiguousarray(scaled.reshape(k // 512, 128, 4, n).transpose(0, 1, 3, 2)).astype(ml_dtypes.float8_e4m3fn).view(np.uint8)
    return words, np.ascontiguousarray(byte.astype(np.uint8).reshape(k // 512, 16, n))


def unpack_weight(words, scales):
    g, p, n, _ = words.shape
    vals = np.ascontiguousarray(words).view(ml_dtypes.float8_e4m3fn).astype(np.float64) * np.repeat(np.exp2(scales.astype(np.float64) - 127.0), 8, axis=1)[..., None]
    return vals.transpose(0, 1, 3, 2).reshape(g * 512, n)


def sigmoid(v):
    return 1.0 / (1.0 + np.exp(-np.maximum(v, -700.0)))

def planes(y):
    n, m = y.shape
    v = y.astype(np.float32).astype(ml_dtypes.bfloat16).astype(np.float64).reshape(n // 32, 32, m)
    top = np.abs(v).max(1)
    byte = np.clip(np.where(top > 0, np.frexp(top)[1] - 1 + 127 - 7, 1), 1, 254)
    codes = (v * np.exp2(127.0 - byte)[:, None, :]).reshape(n, m).astype(np.float32).astype(ml_dtypes.float8_e4m3fn).view(np.uint8)
    words = codes.reshape(n // 512, 128, 4, m).transpose(0, 1, 3, 2)
    return np.ascontiguousarray(words), np.ascontiguousarray(byte.astype(np.uint8).reshape(n // 512, 16, m))


K, T, S, H, G = 512, 1024, 512, 512, 2048


def setup_inputs():
    n = np.random.standard_normal
    s = mx_kscale(K)[:, None]
    packed_xT = pack_weight(n((K, T)) * s)
    packed_w1 = pack_weight(n((K, H)) / np.sqrt(K) / s)
    packed_w2 = pack_weight(n((K, H)) / np.sqrt(K) / s)
    packed_dT = pack_weight(n((K, G)) / s)
    return {
        "x_words": packed_xT[0],
        "x_scales": packed_xT[1],
        "w1_words": packed_w1[0],
        "w1_scales": packed_w1[1],
        "w2_words": packed_w2[0],
        "w2_scales": packed_w2[1],
        "gs": (np.random.uniform(0.5, 1.5, (K, 1)) * s).astype(np.float32),
        "d_words": packed_dT[0],
        "d_scales": packed_dT[1],
        "offs": striped(np.random.permutation(T)[:S]),
        "two": striped(np.random.permutation(T)[:S]),
        "n1": striped8(np.stack([np.random.permutation(S) for _ in range(8)])),
        "n2": striped8(np.stack([np.random.permutation(S) for _ in range(8)])),
        "k1": striped8(np.random.randint(0, G, (8, H))),
        "n3": striped8(np.stack([np.random.permutation(S) for _ in range(8)])),
        "n4": striped8(np.stack([np.random.permutation(S) for _ in range(8)])),
    }


def reference(x_words, x_scales, w1_words, w1_scales, w2_words, w2_scales, gs, d_words, d_scales, offs, two, n1, n2, k1, n3, n4):
    d_k1 = unpack_weight(d_words, d_scales)[np.arange(K)[:, None], runs(k1, K)]
    xq = unpack_weight(x_words, x_scales)[:, unstriped(offs)]
    y = unpack_weight(w1_words, w1_scales).T @ xq
    x_two = unpack_weight(x_words, x_scales)[:, unstriped(two)]
    d = unpack_weight(w2_words, w2_scales).T @ x_two
    z = f64(gs) * (y * (sigmoid(d[np.arange(H)[:, None], runs(n2, H)])) - (0.5 * (y[np.arange(H)[:, None], runs(n1, H)])))
    h = 0.0625 * ((d_k1.T @ mxq(z, 0, "e4m3")))
    out_0 = 0.75 * (h[np.arange(H)[:, None], runs(n3, H)] + h[np.arange(H)[:, None], runs(n4, H)]) - h
    return (out_0,) + planes(out_0)

@@ -1,0 +1,248 @@
+from contextlib import ExitStack
+
+import concourse.mybir as mybir
+
+F32 = mybir.dt.float32
+BF16 = mybir.dt.bfloat16
+I32 = mybir.dt.int32
+U32 = mybir.dt.uint32
+U16 = mybir.dt.uint16
+U8 = mybir.dt.uint8
+FP8X4 = mybir.dt.float8_e4m3fn_x4
+ALU = mybir.AluOpType
+ACT = mybir.ActivationFunctionType
+
+P = 128
+PACK = 4
+T, S, H, G = 1024, 512, 512, 2048
+FLOPS = 3 * 2 * 512 * 512 * 512
+
+Z_CHUNKS = ((0, 256), (256, 256))
+OUT_CHUNKS = ((0, 256), (256, 128), (384, 128))
+
+
+def tile_picked_twqgateblap_none_po_kernel(
+    tc, x_words, x_scales, w1_words, w1_scales, w2_words, w2_scales, gs, d_words, d_scales,
+    offs, two, n1, n2, k1, n3, n4, out_0, out_1, out_2,
+):
+    nc = tc.nc
+    with ExitStack() as ctx:
+        lists = ctx.enter_context(tc.tile_pool(name="lists", bufs=1))
+        keep = ctx.enter_context(tc.tile_pool(name="keep", bufs=1))
+        psum = ctx.enter_context(tc.psum_pool(name="psum", bufs=1))
+
+        def sb(name, shape, dtype):
+            return keep.tile(shape, dtype, name=name, align_bytes=64)
+
+        def load_list(name, dram):
+            tile = lists.tile([P, S // 16], U16, name=name)
+            nc.sync.dma_start(tile[:], dram)
+            return tile
+
+        def load_words(queue, name, dram, width):
+            tile = sb(name, [P, width], U32)
+            queue.dma_start(tile[:].bitcast(I32), dram[0].rearrange("p c r -> p (c r)").bitcast(I32))
+            return tile
+
+        def load_scale_rows(queue, name, dram, width):
+            tile = sb(name, [P, width], U8)
+            rows = dram[0].bitcast(I32).rearrange("(q r) c -> r q c", r=4)
+            for r in range(4):
+                queue.dma_start(
+                    tile[r:P:4, :].bitcast(I32),
+                    rows[r].unsqueeze(1).to_broadcast([4, 8, width // 4]),
+                )
+            return tile
+
+        def entries(tile, start, width):
+            return tile[:, start // 16 : (start + width) // 16]
+
+        def deal(name, tile, dtype, view, run):
+            dealt = sb(name, [P, H], dtype)
+            nc.vector.tensor_copy(
+                dealt[:].bitcast(view).rearrange("p (t a b) -> p a t b", t=PACK, b=run),
+                tile[:].bitcast(view).rearrange("p (a b t) -> p a t b", t=PACK, b=run),
+            )
+            return dealt
+
+        def gather_packed(name, table, offsets, dtype):
+            picked = sb(name, [P, S], dtype)
+            nc.vector.tensor_copy(picked[:], table[:].indirect(offsets[:]))
+            return picked
+
+        def interleave(copy, rounded, planes):
+            copy(
+                rounded[:].rearrange("p (c i) t -> p c t i", i=4),
+                planes[:].rearrange("p t (c i) -> p c t i", i=4),
+            )
+
+        two_l = load_list("two_l", two)
+        xw = load_words(nc.scalar, "xw", x_words, T)
+        w2w = load_words(nc.scalar, "w2w", w2_words, H)
+        xs = load_scale_rows(nc.sync, "xs", x_scales, T)
+        w2s = load_scale_rows(nc.gpsimd, "w2s", w2_scales, H)
+        offs_l = load_list("offs_l", offs)
+        w1w = load_words(nc.sync, "w1w", w1_words, H)
+        w1s = load_scale_rows(nc.sync, "w1s", w1_scales, H)
+        n2_l = load_list("n2_l", n2)
+        k1_l = load_list("k1_l", k1)
+        ds = sb("ds", [P, G], U8)
+        nc.sync.dma_start(
+            ds[:].bitcast(I32), d_scales[0].bitcast(I32).unsqueeze(1).to_broadcast([16, 8, G // 4])
+        )
+        dw = load_words(nc.sync, "dw", d_words, G)
+        gs_t = sb("gs_t", [P, PACK], F32)
+        nc.sync.dma_start(gs_t[:], gs.rearrange("(p t) o -> p (t o)", t=PACK))
+        n1_l = load_list("n1_l", n1)
+        n3_l = load_list("n3_l", n3)
+        n4_l = load_list("n4_l", n4)
+
+        warm = sb("warm", [P, 1], F32)
+        warm_out = sb("warm_out", [P, 1], F32)
+        nc.gpsimd.memset(warm[:], 0.0)
+        nc.scalar.activation(warm_out[:], warm[:], ACT.Sigmoid)
+
+        dk_scale = sb("dk_scale", [P, H], U8)
+        nc.gpsimd.memset(dk_scale[:].bitcast(I32), 0)
+
+        banks = [psum.tile([P, S], F32, name="bank%d" % b) for b in range(8)]
+
+        w2w_d = deal("w2w_d", w2w, U32, I32, 4)
+        x2w = gather_packed("x2w", xw, two_l, U32)
+        x2s = gather_packed("x2s", xs, two_l, U8)
+        w2s_d = deal("w2s_d", w2s, U8, U8, 16)
+
+        def product(bank, cols, lw, ls, t, rw, rs):
+            nc.tensor.matmul_mx(
+                out=bank[:, cols], lhsT=lw[:, P * t : P * (t + 1)].bitcast(FP8X4),
+                lhsT_scale=ls[:, P * t : P * (t + 1)], rhs=rw.bitcast(FP8X4), rhs_scale=rs,
+                start=True, stop=True,
+            )
+
+        whole = slice(0, S)
+        for t in range(PACK):
+            product(banks[t], whole, w2w_d, w2s_d, t, x2w[:], x2s[:])
+
+        x1w = gather_packed("x1w", xw, offs_l, U32)
+        x1s = gather_packed("x1s", xs, offs_l, U8)
+        w1w_d = deal("w1w_d", w1w, U32, I32, 4)
+        w1s_d = deal("w1s_d", w1s, U8, U8, 16)
+        for t in range(PACK):
+            product(banks[PACK + t], whole, w1w_d, w1s_d, t, x1w[:], x1s[:])
+
+        gs_half = sb("gs_half", [P, PACK], F32)
+        nc.gpsimd.tensor_scalar(gs_half[:], gs_t[:], -0.5, 0.0, ALU.mult, ALU.add)
+
+        dks = gather_packed("dks", ds, k1_l, U8)
+        dkw = gather_packed("dkw", dw, k1_l, U32)
+        dks_d = deal("dks_d", dks, U8, U8, 16)
+        dkw_d = deal("dkw_d", dkw, U32, I32, 4)
+        for r in range(4):
+            nc.sync.dma_start(dk_scale[r:P:32, :].bitcast(I32), dks_d[8 * r : P : 32, :].bitcast(I32))
+
+        d_rows = [sb("d_rows%d" % t, [P, S], F32) for t in range(PACK)]
+        y_rows = [sb("y_rows%d" % t, [P, S], F32) for t in range(PACK)]
+        gate = {}
+
+        def sigmoid_gather(c, t):
+            start, width = Z_CHUNKS[c]
+            gate[c, t] = sb("gate%d_%d" % (c, t), [P, width], F32)
+            nc.scalar.activation(gate[c, t][:], d_rows[t][:].indirect(entries(n2_l, start, width)), ACT.Sigmoid)
+
+        for t in range(PACK):
+            nc.scalar.copy(d_rows[t][:], banks[t][:])
+            sigmoid_gather(0, t)
+            nc.scalar.activation(y_rows[t][:], banks[PACK + t][:], ACT.Copy, scale=gs_half[:, t : t + 1])
+        for c in range(1, len(Z_CHUNKS)):
+            for t in range(PACK):
+                sigmoid_gather(c, t)
+
+        h_win = [sb("h_win%d" % t, [P, S], F32) for t in range(PACK)]
+        h_own = [sb("h_own%d" % t, [P, S], F32) for t in range(PACK)]
+
+        def quantise(name, rounded, width):
+            words = sb(name + "_w", [P, width], U32)
+            scale = sb(name + "_s", [P, width], U8)
+            nc.vector.quantize_mx(
+                out=words[:].bitcast(FP8X4), scales=scale[:], in_=rounded[:].rearrange("p c t -> p (c t)")
+            )
+            return words, scale
+
+        def second_product(c, rounded):
+            start, width = Z_CHUNKS[c]
+            cols = slice(start, start + width)
+            zw, zs = quantise("zq%d" % c, rounded, width)
+            for t in range(PACK):
+                product(banks[t], cols, dkw_d, dk_scale, t, zw[:], zs[:])
+            for t in range(PACK):
+                nc.scalar.activation(h_win[t][:, cols], banks[t][:, cols], ACT.Copy, scale=0.75 * 0.0625)
+            for t in range(PACK):
+                nc.scalar.activation(h_own[t][:, cols], banks[t][:, cols], ACT.Copy, scale=0.0625)
+
+        pending = None
+        for c, (start, width) in enumerate(Z_CHUNKS):
+            cols = slice(start, start + width)
+            z = sb("z%d" % c, [P, PACK, width], F32)
+            gated = [sb("gated%d_%d" % (c, t), [P, width], F32) for t in range(PACK)]
+
+            def gate_rows(t):
+                nc.vector.scalar_tensor_tensor(
+                    gated[t][:], y_rows[t][:, cols], -2.0, gate[c, t][:], ALU.mult, ALU.mult
+                )
+
+            gate_rows(0)
+            for t in range(PACK):
+                if t + 1 < PACK:
+                    gate_rows(t + 1)
+                nc.vector.tensor_tensor(
+                    z[:, t, :], y_rows[t][:].indirect(entries(n1_l, start, width)), gated[t][:], ALU.add
+                )
+                if t == 1 and pending is not None:
+                    second_product(*pending)
+            rounded = sb("zb%d" % c, [P, width, PACK], BF16)
+            last = c == len(Z_CHUNKS) - 1
+            interleave(nc.vector.tensor_copy if last else nc.scalar.copy, rounded, z)
+            pending = (c, rounded)
+        second_product(*pending)
+
+        out_rows = out_0.rearrange("(p t) j -> p t j", t=PACK)
+        out_words = out_1[0].rearrange("p c r -> p (c r)").bitcast(I32)
+        out_scale = out_2[0].bitcast(I32)
+
+        def planes_out(c, rounded):
+            start, width = OUT_CHUNKS[c]
+            ow, osc = quantise("oq%d" % c, rounded, width)
+            nc.sync.dma_start(out_words[:, start : start + width], ow[:].bitcast(I32))
+            for q in range(4):
+                queue = nc.sync if q % 2 == 0 else nc.scalar
+                queue.dma_start(
+                    out_scale[4 * q : 4 * q + 4, start // 4 : (start + width) // 4],
+                    osc[32 * q : 32 * q + 4, :].bitcast(I32),
+                )
+
+        pending = None
+        for c, (start, width) in enumerate(OUT_CHUNKS):
+            cols = slice(start, start + width)
+            o = sb("o%d" % c, [P, PACK, width], F32)
+            part = [sb("part%d_%d" % (c, t), [P, width], F32) for t in range(PACK)]
+
+            def first(t):
+                nc.vector.tensor_tensor(
+                    part[t][:], h_win[t][:].indirect(entries(n3_l, start, width)), h_own[t][:, cols], ALU.subtract
+                )
+
+            first(0)
+            for t in range(PACK):
+                if t + 1 < PACK:
+                    first(t + 1)
+                nc.vector.tensor_tensor(
+                    o[:, t, :], h_win[t][:].indirect(entries(n4_l, start, width)), part[t][:], ALU.add
+                )
+                if t == 1 and pending is not None:
+                    planes_out(*pending)
+            nc.sync.dma_start(out_rows[:, :, cols], o[:])
+            rounded = sb("ob%d" % c, [P, width, PACK], BF16)
+            last = c == len(OUT_CHUNKS) - 1
+            interleave(nc.vector.tensor_copy if last else nc.scalar.copy, rounded, o)
+            pending = (c, rounded)
+        planes_out(*pending)

@@ -18,6 +18,7 @@ T, S, H, G = 1024, 512, 512, 2048
 FLOPS = 3 * 2 * 512 * 512 * 512
 
 Z_CHUNKS = ((0, 256), (256, 256))
+GATE_HALF = 256
 OUT_CHUNKS = ((0, 256), (256, 128), (384, 128))
 
 
@@ -29,10 +30,13 @@ def tile_picked_twqgateblap_none_po_kernel(
     with ExitStack() as ctx:
         lists = ctx.enter_context(tc.tile_pool(name="lists", bufs=1))
         keep = ctx.enter_context(tc.tile_pool(name="keep", bufs=1))
+        shared = ctx.enter_context(tc.tile_pool(name="shared", bufs=1))
         psum = ctx.enter_context(tc.psum_pool(name="psum", bufs=1))
 
-        def sb(name, shape, dtype):
-            return keep.tile(shape, dtype, name=name, align_bytes=64)
+        def sb(name, shape, dtype, offset=None):
+            if offset is None:
+                return keep.tile(shape, dtype, name=name, align_bytes=64)
+            return shared.tile(shape, dtype, name=name, align_bytes=64, offset=offset)
 
         def load_list(name, dram):
             tile = lists.tile([P, S // 16], U16, name=name)
@@ -44,73 +48,85 @@ def tile_picked_twqgateblap_none_po_kernel(
             queue.dma_start(tile[:].bitcast(I32), dram[0].rearrange("p c r -> p (c r)").bitcast(I32))
             return tile
 
-        def load_scale_rows(queue, name, dram, width):
-            tile = sb(name, [P, width], U8)
-            rows = dram[0].bitcast(I32).rearrange("(q r) c -> r q c", r=4)
-            for r in range(4):
-                queue.dma_start(
-                    tile[r:P:4, :].bitcast(I32),
-                    rows[r].unsqueeze(1).to_broadcast([4, 8, width // 4]),
-                )
+        def zeroed(name, width, offset=None):
+            tile = sb(name, [P, width], U8, offset)
+            nc.gpsimd.memset(tile[:].bitcast(I32), 0)
             return tile
+
+        def load_scale_rows(queue, tile, dram):
+            rows = dram[0].bitcast(I32).rearrange("(q r) c -> q r c", r=4)
+            for q in range(4):
+                queue.dma_start(
+                    tile[32 * q : 32 * q + 4, :].bitcast(I32),
+                    rows[q],
+                )
+
+        def load_scale_rows_repeated(queues, tile, dram, width):
+            rows = dram[0].bitcast(I32).rearrange("(q r) c -> q r c", r=4)
+            for q in range(4):
+                queues[q].dma_start(
+                    tile[32 * q : 32 * q + 32, :].bitcast(I32),
+                    rows[q].unsqueeze(0).to_broadcast([8, 4, width // 4]),
+                )
 
         def entries(tile, start, width):
             return tile[:, start // 16 : (start + width) // 16]
 
-        def deal(name, tile, dtype, view, run):
-            dealt = sb(name, [P, H], dtype)
+        def deal(name, tile, dtype, view, run, offset=None):
+            dealt = sb(name, [P, H], dtype, offset)
             nc.vector.tensor_copy(
                 dealt[:].bitcast(view).rearrange("p (t a b) -> p a t b", t=PACK, b=run),
                 tile[:].bitcast(view).rearrange("p (a b t) -> p a t b", t=PACK, b=run),
             )
             return dealt
 
-        def gather_packed(name, table, offsets, dtype):
-            picked = sb(name, [P, S], dtype)
+        def gather_packed(name, table, offsets, dtype, offset=None):
+            picked = sb(name, [P, S], dtype, offset)
             nc.vector.tensor_copy(picked[:], table[:].indirect(offsets[:]))
             return picked
 
         def interleave(copy, rounded, planes):
             copy(
-                rounded[:].rearrange("p (c i) t -> p c t i", i=4),
-                planes[:].rearrange("p t (c i) -> p c t i", i=4),
+                rounded.rearrange("p (c i) t -> p c t i", i=4),
+                planes.rearrange("p t (c i) -> p c t i", i=4),
             )
 
-        two_l = load_list("two_l", two)
-        xw = load_words(nc.scalar, "xw", x_words, T)
-        w2w = load_words(nc.scalar, "w2w", w2_words, H)
-        xs = load_scale_rows(nc.sync, "xs", x_scales, T)
-        w2s = load_scale_rows(nc.gpsimd, "w2s", w2_scales, H)
-        offs_l = load_list("offs_l", offs)
-        w1w = load_words(nc.sync, "w1w", w1_words, H)
-        w1s = load_scale_rows(nc.sync, "w1s", w1_scales, H)
-        n2_l = load_list("n2_l", n2)
-        k1_l = load_list("k1_l", k1)
-        ds = sb("ds", [P, G], U8)
-        nc.sync.dma_start(
-            ds[:].bitcast(I32), d_scales[0].bitcast(I32).unsqueeze(1).to_broadcast([16, 8, G // 4])
-        )
-        dw = load_words(nc.sync, "dw", d_words, G)
-        gs_t = sb("gs_t", [P, PACK], F32)
-        nc.sync.dma_start(gs_t[:], gs.rearrange("(p t) o -> p (t o)", t=PACK))
-        n1_l = load_list("n1_l", n1)
-        n3_l = load_list("n3_l", n3)
-        n4_l = load_list("n4_l", n4)
+        w1s = zeroed("w1s", H, offset=4 * S - H // 2)
+        w2s = zeroed("w2s", H)
+        ds = zeroed("ds", G)
+        dk_scale = zeroed("dk_scale", H)
 
         warm = sb("warm", [P, 1], F32)
         warm_out = sb("warm_out", [P, 1], F32)
         nc.gpsimd.memset(warm[:], 0.0)
-        nc.scalar.activation(warm_out[:], warm[:], ACT.Sigmoid)
 
-        dk_scale = sb("dk_scale", [P, H], U8)
-        nc.gpsimd.memset(dk_scale[:].bitcast(I32), 0)
+        xw = load_words(nc.scalar, "xw", x_words, T)
+        offs_l = load_list("offs_l", offs)
+        two_l = load_list("two_l", two)
+        xs = sb("xs", [P, T], U8)
+        load_scale_rows_repeated((nc.sync, nc.scalar, nc.sync, nc.scalar), xs, x_scales, T)
+        w1w = load_words(nc.sync, "w1w", w1_words, H)
+        load_scale_rows(nc.sync, w1s, w1_scales)
+        n2_l = load_list("n2_l", n2)
+        w2w = load_words(nc.sync, "w2w", w2_words, H)
+        gs_t = sb("gs_t", [P, PACK], F32)
+        nc.sync.dma_start(gs_t[:], gs.rearrange("(p t) o -> p (t o)", t=PACK))
+        dw = load_words(nc.sync, "dw", d_words, G)
+        load_scale_rows(nc.sync, w2s, w2_scales)
+        k1_l = load_list("k1_l", k1)
+        nc.sync.dma_start(ds[0:P:8, :].bitcast(I32), d_scales[0].bitcast(I32))
+        n1_l = load_list("n1_l", n1)
+        n3_l = load_list("n3_l", n3)
+        n4_l = load_list("n4_l", n4)
+
+        nc.scalar.activation(warm_out[:], warm[:], ACT.Sigmoid)
 
         banks = [psum.tile([P, S], F32, name="bank%d" % b) for b in range(8)]
 
-        w2w_d = deal("w2w_d", w2w, U32, I32, 4)
-        x2w = gather_packed("x2w", xw, two_l, U32)
-        x2s = gather_packed("x2s", xs, two_l, U8)
-        w2s_d = deal("w2s_d", w2s, U8, U8, 16)
+        x1w = gather_packed("x1w", xw, offs_l, U32)
+        x1s = gather_packed("x1s", xs, offs_l, U8)
+        w1w_d = deal("w1w_d", w1w, U32, I32, 4)
+        w1s_d = deal("w1s_d", w1s, U8, U8, 16)
 
         def product(bank, cols, lw, ls, t, rw, rs):
             nc.tensor.matmul_mx(
@@ -121,24 +137,26 @@ def tile_picked_twqgateblap_none_po_kernel(
 
         whole = slice(0, S)
         for t in range(PACK):
-            product(banks[t], whole, w2w_d, w2s_d, t, x2w[:], x2s[:])
-
-        x1w = gather_packed("x1w", xw, offs_l, U32)
-        x1s = gather_packed("x1s", xs, offs_l, U8)
-        w1w_d = deal("w1w_d", w1w, U32, I32, 4)
-        w1s_d = deal("w1s_d", w1s, U8, U8, 16)
-        for t in range(PACK):
             product(banks[PACK + t], whole, w1w_d, w1s_d, t, x1w[:], x1s[:])
 
+        x2w = gather_packed("x2w", xw, two_l, U32, offset=0)
+        x2s = gather_packed("x2s", xs, two_l, U8, offset=4 * S)
+        w2w_d = deal("w2w_d", w2w, U32, I32, 4, offset=5 * S)
+        w2s_d = deal("w2s_d", w2s, U8, U8, 16)
+        for t in range(PACK):
+            product(banks[t], whole, w2w_d, w2s_d, t, x2w[:], x2s[:])
+
         gs_half = sb("gs_half", [P, PACK], F32)
-        nc.gpsimd.tensor_scalar(gs_half[:], gs_t[:], -0.5, 0.0, ALU.mult, ALU.add)
+        nc.scalar.activation(gs_half[:], gs_t[:], ACT.Copy, scale=-0.5)
 
         dks = gather_packed("dks", ds, k1_l, U8)
         dkw = gather_packed("dkw", dw, k1_l, U32)
         dks_d = deal("dks_d", dks, U8, U8, 16)
         dkw_d = deal("dkw_d", dkw, U32, I32, 4)
-        for r in range(4):
-            nc.sync.dma_start(dk_scale[r:P:32, :].bitcast(I32), dks_d[8 * r : P : 32, :].bitcast(I32))
+        for q in range(4):
+            nc.sync.dma_start(
+                dk_scale[32 * q : 32 * q + 4, :].bitcast(I32), dks_d[32 * q : 32 * q + 32 : 8, :].bitcast(I32)
+            )
 
         d_rows = [sb("d_rows%d" % t, [P, S], F32) for t in range(PACK)]
         y_rows = [sb("y_rows%d" % t, [P, S], F32) for t in range(PACK)]
@@ -146,13 +164,17 @@ def tile_picked_twqgateblap_none_po_kernel(
 
         def sigmoid_gather(c, t):
             start, width = Z_CHUNKS[c]
-            gate[c, t] = sb("gate%d_%d" % (c, t), [P, width], F32)
+            offset = None if c == 0 else 4 * (GATE_HALF * t + start - GATE_HALF)
+            gate[c, t] = sb("gate%d_%d" % (c, t), [P, width], F32, offset)
             nc.scalar.activation(gate[c, t][:], d_rows[t][:].indirect(entries(n2_l, start, width)), ACT.Sigmoid)
 
         for t in range(PACK):
-            nc.scalar.copy(d_rows[t][:], banks[t][:])
-            sigmoid_gather(0, t)
             nc.scalar.activation(y_rows[t][:], banks[PACK + t][:], ACT.Copy, scale=gs_half[:, t : t + 1])
+        nc.scalar.copy(d_rows[0][:], banks[0][:])
+        for t in range(PACK):
+            if t + 1 < PACK:
+                nc.scalar.copy(d_rows[t + 1][:], banks[t + 1][:])
+            sigmoid_gather(0, t)
         for c in range(1, len(Z_CHUNKS)):
             for t in range(PACK):
                 sigmoid_gather(c, t)
@@ -160,24 +182,42 @@ def tile_picked_twqgateblap_none_po_kernel(
         h_win = [sb("h_win%d" % t, [P, S], F32) for t in range(PACK)]
         h_own = [sb("h_own%d" % t, [P, S], F32) for t in range(PACK)]
 
-        def quantise(name, rounded, width):
-            words = sb(name + "_w", [P, width], U32)
-            scale = sb(name + "_s", [P, width], U8)
+        def quantise(words, scale, rounded):
             nc.vector.quantize_mx(
-                out=words[:].bitcast(FP8X4), scales=scale[:], in_=rounded[:].rearrange("p c t -> p (c t)")
+                out=words.bitcast(FP8X4), scales=scale, in_=rounded[:].rearrange("p c t -> p (c t)")
             )
-            return words, scale
+
+        def round_on_scalar(name, planes, width):
+            rounded = sb(name, [P, width, PACK], BF16)
+            interleave(nc.scalar.copy, rounded[:], planes[:])
+            return [rounded]
+
+        def round_on_vector(name, planes, width):
+            halves = [sb("%s_%d" % (name, u), [P, width // 2, PACK], BF16) for u in range(2)]
+            for u in range(2):
+                interleave(nc.vector.tensor_copy, halves[u][:], planes[:, :, u * width // 2 : (u + 1) * width // 2])
+            return halves
+
+        def quantise_pieces(words, scale, pieces, start, width):
+            step = width // len(pieces)
+            for u, piece in enumerate(pieces):
+                cols = slice(start + u * step, start + (u + 1) * step)
+                quantise(words[:, cols], scale[:, cols], piece)
+
+        def h_bank(c, t):
+            return banks[PACK * (1 - c) + t]
 
         def second_product(c, rounded):
             start, width = Z_CHUNKS[c]
-            cols = slice(start, start + width)
-            zw, zs = quantise("zq%d" % c, rounded, width)
+            zw = sb("zw%d" % c, [P, width], U32)
+            zs = sb("zs%d" % c, [P, width], U8)
+            quantise_pieces(zw, zs, rounded, 0, width)
             for t in range(PACK):
-                product(banks[t], cols, dkw_d, dk_scale, t, zw[:], zs[:])
-            for t in range(PACK):
-                nc.scalar.activation(h_win[t][:, cols], banks[t][:, cols], ACT.Copy, scale=0.75 * 0.0625)
-            for t in range(PACK):
-                nc.scalar.activation(h_own[t][:, cols], banks[t][:, cols], ACT.Copy, scale=0.0625)
+                product(h_bank(c, t), slice(0, width), dkw_d, dk_scale, t, zw[:], zs[:])
+
+        def h_out(rows, factor, c, t):
+            start, width = Z_CHUNKS[c]
+            nc.scalar.activation(rows[t][:, start : start + width], h_bank(c, t)[:, 0:width], ACT.Copy, scale=factor)
 
         pending = None
         for c, (start, width) in enumerate(Z_CHUNKS):
@@ -197,28 +237,31 @@ def tile_picked_twqgateblap_none_po_kernel(
                 nc.vector.tensor_tensor(
                     z[:, t, :], y_rows[t][:].indirect(entries(n1_l, start, width)), gated[t][:], ALU.add
                 )
-                if t == 1 and pending is not None:
+                if t == 2 and pending is not None:
                     second_product(*pending)
-            rounded = sb("zb%d" % c, [P, width, PACK], BF16)
             last = c == len(Z_CHUNKS) - 1
-            interleave(nc.vector.tensor_copy if last else nc.scalar.copy, rounded, z)
-            pending = (c, rounded)
+            pending = (c, (round_on_vector if last else round_on_scalar)("zb%d" % c, z, width))
         second_product(*pending)
+
+        for t in range(PACK):
+            h_out(h_win, 0.75 * 0.0625, 0, t)
+        for t in range(PACK):
+            h_out(h_win, 0.75 * 0.0625, 1, t)
+            h_out(h_own, 0.0625, 0, t)
+        for t in range(PACK):
+            h_out(h_own, 0.0625, 1, t)
 
         out_rows = out_0.rearrange("(p t) j -> p t j", t=PACK)
         out_words = out_1[0].rearrange("p c r -> p (c r)").bitcast(I32)
         out_scale = out_2[0].bitcast(I32)
 
+        o_words = sb("o_words", [P, S], U32)
+        o_scale = sb("o_scale", [P, S], U8)
+
         def planes_out(c, rounded):
             start, width = OUT_CHUNKS[c]
-            ow, osc = quantise("oq%d" % c, rounded, width)
-            nc.sync.dma_start(out_words[:, start : start + width], ow[:].bitcast(I32))
-            for q in range(4):
-                queue = nc.sync if q % 2 == 0 else nc.scalar
-                queue.dma_start(
-                    out_scale[4 * q : 4 * q + 4, start // 4 : (start + width) // 4],
-                    osc[32 * q : 32 * q + 4, :].bitcast(I32),
-                )
+            quantise_pieces(o_words, o_scale, rounded, start, width)
+            nc.sync.dma_start(out_words[:, start : start + width], o_words[:, start : start + width].bitcast(I32))
 
         pending = None
         for c, (start, width) in enumerate(OUT_CHUNKS):
@@ -241,8 +284,9 @@ def tile_picked_twqgateblap_none_po_kernel(
                 if t == 1 and pending is not None:
                     planes_out(*pending)
             nc.sync.dma_start(out_rows[:, :, cols], o[:])
-            rounded = sb("ob%d" % c, [P, width, PACK], BF16)
             last = c == len(OUT_CHUNKS) - 1
-            interleave(nc.vector.tensor_copy if last else nc.scalar.copy, rounded, o)
-            pending = (c, rounded)
+            pending = (c, (round_on_vector if last else round_on_scalar)("ob%d" % c, o, width))
         planes_out(*pending)
+        for q in range(4):
+            queue = nc.scalar if q % 2 == 0 else nc.sync
+            queue.dma_start(out_scale[4 * q : 4 * q + 4, :], o_scale[32 * q : 32 * q + 4, :].bitcast(I32))

from contextlib import ExitStack

import concourse.mybir as mybir

F32 = mybir.dt.float32
BF16 = mybir.dt.bfloat16
I32 = mybir.dt.int32
U32 = mybir.dt.uint32
U16 = mybir.dt.uint16
U8 = mybir.dt.uint8
FP8X4 = mybir.dt.float8_e4m3fn_x4
ALU = mybir.AluOpType
ACT = mybir.ActivationFunctionType

P = 128
PACK = 4
T, S, H, G = 1024, 512, 512, 2048
FLOPS = 3 * 2 * 512 * 512 * 512

Z_CHUNKS = ((0, 256), (256, 256))
GATE_HALF = 256
OUT_CHUNKS = ((0, 256), (256, 128), (384, 128))


def tile_picked_twqgateblap_none_po_kernel(
    tc, x_words, x_scales, w1_words, w1_scales, w2_words, w2_scales, gs, d_words, d_scales,
    offs, two, n1, n2, k1, n3, n4, out_0, out_1, out_2,
):
    nc = tc.nc
    with ExitStack() as ctx:
        lists = ctx.enter_context(tc.tile_pool(name="lists", bufs=1))
        keep = ctx.enter_context(tc.tile_pool(name="keep", bufs=1))
        shared = ctx.enter_context(tc.tile_pool(name="shared", bufs=1))
        psum = ctx.enter_context(tc.psum_pool(name="psum", bufs=1))

        def sb(name, shape, dtype, offset=None):
            if offset is None:
                return keep.tile(shape, dtype, name=name, align_bytes=64)
            return shared.tile(shape, dtype, name=name, align_bytes=64, offset=offset)

        def load_list(name, dram):
            tile = lists.tile([P, S // 16], U16, name=name)
            nc.sync.dma_start(tile[:], dram)
            return tile

        def load_words(queue, name, dram, width):
            tile = sb(name, [P, width], U32)
            queue.dma_start(tile[:].bitcast(I32), dram[0].rearrange("p c r -> p (c r)").bitcast(I32))
            return tile

        def zeroed(name, width, offset=None):
            tile = sb(name, [P, width], U8, offset)
            nc.gpsimd.memset(tile[:].bitcast(I32), 0)
            return tile

        def load_scale_rows(queue, tile, dram):
            rows = dram[0].bitcast(I32).rearrange("(q r) c -> q r c", r=4)
            for q in range(4):
                queue.dma_start(
                    tile[32 * q : 32 * q + 4, :].bitcast(I32),
                    rows[q],
                )

        def load_scale_rows_repeated(queues, tile, dram, width):
            rows = dram[0].bitcast(I32).rearrange("(q r) c -> q r c", r=4)
            for q in range(4):
                queues[q].dma_start(
                    tile[32 * q : 32 * q + 32, :].bitcast(I32),
                    rows[q].unsqueeze(0).to_broadcast([8, 4, width // 4]),
                )

        def entries(tile, start, width):
            return tile[:, start // 16 : (start + width) // 16]

        def deal(name, tile, dtype, view, run, offset=None):
            dealt = sb(name, [P, H], dtype, offset)
            nc.vector.tensor_copy(
                dealt[:].bitcast(view).rearrange("p (t a b) -> p a t b", t=PACK, b=run),
                tile[:].bitcast(view).rearrange("p (a b t) -> p a t b", t=PACK, b=run),
            )
            return dealt

        def gather_packed(name, table, offsets, dtype, offset=None):
            picked = sb(name, [P, S], dtype, offset)
            nc.vector.tensor_copy(picked[:], table[:].indirect(offsets[:]))
            return picked

        def interleave(copy, rounded, planes):
            copy(
                rounded.rearrange("p (c i) t -> p c t i", i=4),
                planes.rearrange("p t (c i) -> p c t i", i=4),
            )

        w1s = zeroed("w1s", H, offset=4 * S - H // 2)
        w2s = zeroed("w2s", H)
        ds = zeroed("ds", G)
        dk_scale = zeroed("dk_scale", H)

        warm = sb("warm", [P, 1], F32)
        warm_out = sb("warm_out", [P, 1], F32)
        nc.gpsimd.memset(warm[:], 0.0)

        xw = load_words(nc.scalar, "xw", x_words, T)
        offs_l = load_list("offs_l", offs)
        two_l = load_list("two_l", two)
        xs = sb("xs", [P, T], U8)
        load_scale_rows_repeated((nc.sync, nc.scalar, nc.sync, nc.scalar), xs, x_scales, T)
        w1w = load_words(nc.sync, "w1w", w1_words, H)
        load_scale_rows(nc.sync, w1s, w1_scales)
        n2_l = load_list("n2_l", n2)
        w2w = load_words(nc.sync, "w2w", w2_words, H)
        gs_t = sb("gs_t", [P, PACK], F32)
        nc.sync.dma_start(gs_t[:], gs.rearrange("(p t) o -> p (t o)", t=PACK))
        dw = load_words(nc.sync, "dw", d_words, G)
        load_scale_rows(nc.sync, w2s, w2_scales)
        k1_l = load_list("k1_l", k1)
        nc.sync.dma_start(ds[0:P:8, :].bitcast(I32), d_scales[0].bitcast(I32))
        n1_l = load_list("n1_l", n1)
        n3_l = load_list("n3_l", n3)
        n4_l = load_list("n4_l", n4)

        nc.scalar.activation(warm_out[:], warm[:], ACT.Sigmoid)

        banks = [psum.tile([P, S], F32, name="bank%d" % b) for b in range(8)]

        x1w = gather_packed("x1w", xw, offs_l, U32)
        x1s = gather_packed("x1s", xs, offs_l, U8)
        w1w_d = deal("w1w_d", w1w, U32, I32, 4)
        w1s_d = deal("w1s_d", w1s, U8, U8, 16)

        def product(bank, cols, lw, ls, t, rw, rs):
            nc.tensor.matmul_mx(
                out=bank[:, cols], lhsT=lw[:, P * t : P * (t + 1)].bitcast(FP8X4),
                lhsT_scale=ls[:, P * t : P * (t + 1)], rhs=rw.bitcast(FP8X4), rhs_scale=rs,
                start=True, stop=True,
            )

        whole = slice(0, S)
        for t in range(PACK):
            product(banks[PACK + t], whole, w1w_d, w1s_d, t, x1w[:], x1s[:])

        x2w = gather_packed("x2w", xw, two_l, U32, offset=0)
        x2s = gather_packed("x2s", xs, two_l, U8, offset=4 * S)
        w2w_d = deal("w2w_d", w2w, U32, I32, 4, offset=5 * S)
        w2s_d = deal("w2s_d", w2s, U8, U8, 16)
        for t in range(PACK):
            product(banks[t], whole, w2w_d, w2s_d, t, x2w[:], x2s[:])

        gs_half = sb("gs_half", [P, PACK], F32)
        nc.scalar.activation(gs_half[:], gs_t[:], ACT.Copy, scale=-0.5)

        dks = gather_packed("dks", ds, k1_l, U8)
        dkw = gather_packed("dkw", dw, k1_l, U32)
        dks_d = deal("dks_d", dks, U8, U8, 16)
        dkw_d = deal("dkw_d", dkw, U32, I32, 4)
        for q in range(4):
            nc.sync.dma_start(
                dk_scale[32 * q : 32 * q + 4, :].bitcast(I32), dks_d[32 * q : 32 * q + 32 : 8, :].bitcast(I32)
            )

        d_rows = [sb("d_rows%d" % t, [P, S], F32) for t in range(PACK)]
        y_rows = [sb("y_rows%d" % t, [P, S], F32) for t in range(PACK)]
        gate = {}

        def sigmoid_gather(c, t):
            start, width = Z_CHUNKS[c]
            offset = None if c == 0 else 4 * (GATE_HALF * t + start - GATE_HALF)
            gate[c, t] = sb("gate%d_%d" % (c, t), [P, width], F32, offset)
            nc.scalar.activation(gate[c, t][:], d_rows[t][:].indirect(entries(n2_l, start, width)), ACT.Sigmoid)

        for t in range(PACK):
            nc.scalar.activation(y_rows[t][:], banks[PACK + t][:], ACT.Copy, scale=gs_half[:, t : t + 1])
        nc.scalar.copy(d_rows[0][:], banks[0][:])
        for t in range(PACK):
            if t + 1 < PACK:
                nc.scalar.copy(d_rows[t + 1][:], banks[t + 1][:])
            sigmoid_gather(0, t)
        for c in range(1, len(Z_CHUNKS)):
            for t in range(PACK):
                sigmoid_gather(c, t)

        h_win = [sb("h_win%d" % t, [P, S], F32) for t in range(PACK)]
        h_own = [sb("h_own%d" % t, [P, S], F32) for t in range(PACK)]

        def quantise(words, scale, rounded):
            nc.vector.quantize_mx(
                out=words.bitcast(FP8X4), scales=scale, in_=rounded[:].rearrange("p c t -> p (c t)")
            )

        def round_on_scalar(name, planes, width):
            rounded = sb(name, [P, width, PACK], BF16)
            interleave(nc.scalar.copy, rounded[:], planes[:])
            return [rounded]

        def round_on_vector(name, planes, width):
            halves = [sb("%s_%d" % (name, u), [P, width // 2, PACK], BF16) for u in range(2)]
            for u in range(2):
                interleave(nc.vector.tensor_copy, halves[u][:], planes[:, :, u * width // 2 : (u + 1) * width // 2])
            return halves

        def quantise_pieces(words, scale, pieces, start, width):
            step = width // len(pieces)
            for u, piece in enumerate(pieces):
                cols = slice(start + u * step, start + (u + 1) * step)
                quantise(words[:, cols], scale[:, cols], piece)

        def h_bank(c, t):
            return banks[PACK * (1 - c) + t]

        def second_product(c, rounded):
            start, width = Z_CHUNKS[c]
            zw = sb("zw%d" % c, [P, width], U32)
            zs = sb("zs%d" % c, [P, width], U8)
            quantise_pieces(zw, zs, rounded, 0, width)
            for t in range(PACK):
                product(h_bank(c, t), slice(0, width), dkw_d, dk_scale, t, zw[:], zs[:])

        def h_out(rows, factor, c, t):
            start, width = Z_CHUNKS[c]
            nc.scalar.activation(rows[t][:, start : start + width], h_bank(c, t)[:, 0:width], ACT.Copy, scale=factor)

        pending = None
        for c, (start, width) in enumerate(Z_CHUNKS):
            cols = slice(start, start + width)
            z = sb("z%d" % c, [P, PACK, width], F32)
            gated = [sb("gated%d_%d" % (c, t), [P, width], F32) for t in range(PACK)]

            def gate_rows(t):
                nc.vector.scalar_tensor_tensor(
                    gated[t][:], y_rows[t][:, cols], -2.0, gate[c, t][:], ALU.mult, ALU.mult
                )

            gate_rows(0)
            for t in range(PACK):
                if t + 1 < PACK:
                    gate_rows(t + 1)
                nc.vector.tensor_tensor(
                    z[:, t, :], y_rows[t][:].indirect(entries(n1_l, start, width)), gated[t][:], ALU.add
                )
                if t == 2 and pending is not None:
                    second_product(*pending)
            last = c == len(Z_CHUNKS) - 1
            pending = (c, (round_on_vector if last else round_on_scalar)("zb%d" % c, z, width))
        second_product(*pending)

        for t in range(PACK):
            h_out(h_win, 0.75 * 0.0625, 0, t)
        for t in range(PACK):
            h_out(h_win, 0.75 * 0.0625, 1, t)
            h_out(h_own, 0.0625, 0, t)
        for t in range(PACK):
            h_out(h_own, 0.0625, 1, t)

        out_rows = out_0.rearrange("(p t) j -> p t j", t=PACK)
        out_words = out_1[0].rearrange("p c r -> p (c r)").bitcast(I32)
        out_scale = out_2[0].bitcast(I32)

        o_words = sb("o_words", [P, S], U32)
        o_scale = sb("o_scale", [P, S], U8)

        def planes_out(c, rounded):
            start, width = OUT_CHUNKS[c]
            quantise_pieces(o_words, o_scale, rounded, start, width)
            nc.sync.dma_start(out_words[:, start : start + width], o_words[:, start : start + width].bitcast(I32))

        pending = None
        for c, (start, width) in enumerate(OUT_CHUNKS):
            cols = slice(start, start + width)
            o = sb("o%d" % c, [P, PACK, width], F32)
            part = [sb("part%d_%d" % (c, t), [P, width], F32) for t in range(PACK)]

            def first(t):
                nc.vector.tensor_tensor(
                    part[t][:], h_win[t][:].indirect(entries(n3_l, start, width)), h_own[t][:, cols], ALU.subtract
                )

            first(0)
            for t in range(PACK):
                if t + 1 < PACK:
                    first(t + 1)
                nc.vector.tensor_tensor(
                    o[:, t, :], h_win[t][:].indirect(entries(n4_l, start, width)), part[t][:], ALU.add
                )
                if t == 1 and pending is not None:
                    planes_out(*pending)
            nc.sync.dma_start(out_rows[:, :, cols], o[:])
            last = c == len(OUT_CHUNKS) - 1
            pending = (c, (round_on_vector if last else round_on_scalar)("ob%d" % c, o, width))
        planes_out(*pending)
        for q in range(4):
            queue = nc.scalar if q % 2 == 0 else nc.sync
            queue.dma_start(out_scale[4 * q : 4 * q + 4, :], o_scale[32 * q : 32 * q + 4, :].bitcast(I32))
